import numpy as np, ml_dtypes
CORES = [32,40,48,56,64,72,80,88,96,104,112,120]
N = 12
F = 256
GROUPS = [[0,3,6,9],[1,4,7,10],[2,5,8,11]]
def setup_inputs(rng):
    return {"x": rng.standard_normal((N, 128, F), dtype=np.float32).astype(ml_dtypes.bfloat16), "w": (rng.standard_normal((N, 128, 128), dtype=np.float32) / 11).astype(ml_dtypes.bfloat16)}
def setup_inputs_big(rng):
    d = setup_inputs(rng)
    for k in ("x", "w"): d[k] = (d[k].astype(np.float32) * 1024.0).astype(d[k].dtype)
    return d
def setup_inputs_small(rng):
    d = setup_inputs(rng)
    for k in ("x", "w"): d[k] = (d[k].astype(np.float32) * (1 / 1024.0)).astype(d[k].dtype)
    return d
def setup_inputs_apart(rng):
    d = setup_inputs(rng)
    f = (10.0 ** rng.permutation(np.linspace(-1.5, 1.5, N))).astype(np.float32).reshape(N, 1, 1)
    for k in ("x", "w"): d[k] = (d[k].astype(np.float32) * f).astype(d[k].dtype)
    return d
def reference(x, w):
    X, W = x.astype(np.float64), w.astype(np.float64)
    s = sum(W[g[0]].T @ np.maximum(sum(X[j] for j in g), 0.0) for g in GROUPS).astype(ml_dtypes.bfloat16)
    return {"y": np.broadcast_to(s, (N,) + s.shape)}

@@ -1,0 +1,188 @@
+from concourse.bass import DstId, RemoteDMATransfer
+from concourse.mybir import AluOpType
+
+P = 128
+F = 256
+M = 128
+G = 3
+MEM = 2
+K = 2
+NC = F // K
+
+SCRATCH = {
+    "xs": ("sbuf", [P, F], "bfloat16"),
+    "ws": ("sbuf", [P, M], "bfloat16"),
+    "ys": ("sbuf", [P, F], "bfloat16"),
+    "land": ("sbuf", [P, MEM * G * NC], "bfloat16"),
+    "part": ("sbuf", [P, G * NC], "bfloat16"),
+    "wall": ("sbuf", [P, G * M], "bfloat16"),
+    "zero": ("sbuf", [P, G * NC], "bfloat16"),
+    "own": ("sbuf", [P, G * NC], "bfloat16"),
+    "top": ("sbuf", [P, G * NC], "bfloat16"),
+    "res": ("sbuf", [P, NC], "bfloat16"),
+    "neg": ("psum", [P, 512], "float32"),
+    "acc": ("psum", [P, 512], "float32"),
+}
+SEMAPHORES = ["xld", "wld", "st", "sent", "xarr", "wown", "wmate", "carr", "yarr",
+              "vz", "va", "vn", "vt", "mm", "vr"]
+
+
+def _plan(T, topo):
+    cores = list(T.cores)
+    groups = T.tables["GROUPS"]
+    chips = [topo.chip(c) for c in cores]
+    reps = []
+    pl = []
+    for ch in chips:
+        hit = [i for i, r in enumerate(reps) if r == ch or topo.same_plane(r, ch)]
+        if not hit:
+            reps.append(ch)
+            hit = [len(reps) - 1]
+        pl.append(hit[0])
+    assert len(reps) == 2
+    pairs = [(a, b) for a in range(len(cores)) if pl[a] == 0
+             for b in range(len(cores)) if topo.mates(chips[a], chips[b])]
+    every = range(topo.CHIPS * topo.CORES_PER_CHIP)
+    workers = []
+    for a, b in pairs[:K]:
+        two = []
+        for r, q in ((a, b), (b, a)):
+            two.append([c for c in every
+                        if topo.chip(c) == chips[r] and T.rank_of(c) is None
+                        and topo.may_write(c, cores[q]) and topo.die(c) == topo.die(cores[r])][0])
+        workers.append(two)
+    order = sorted(range(len(groups)), key=lambda gi: (pl[groups[gi][0]], gi))
+    wslot = [order.index(gi) for gi in range(len(groups))]
+    return cores, groups, pl, workers, wslot
+
+
+def rank_program(g, core, T, topo):
+    cores, groups, pl, workers, wslot = _plan(T, topo)
+    S = T.sem
+
+    def did(c):
+        rid, pid, _ = topo.addr(c)
+        return DstId(rid=rid, pnc=pid)
+
+    def common(src, dsts):
+        m = topo.mask(src, dsts[0])
+        for d in dsts[1:]:
+            m &= topo.mask(src, d)
+        return [e for e in range(m.bit_length()) if (m >> e) & 1]
+
+    def bits(es):
+        return sum(1 << e for e in es)
+
+    rank = T.rank_of(core)
+
+    if rank is not None:
+        p = pl[rank]
+        gi = [i for i, gr in enumerate(groups) if rank in gr][0]
+        mem = [j for j in groups[gi] if pl[j] == p].index(rank)
+        first = groups[gi][0] == rank
+        mine = [workers[k][p] for k in range(K)]
+        es = common(core, mine)
+        per = len(es) // K
+
+        g.sync.dma_start(T.xs[:], T.x[:]).then_inc(S.xld, 16)
+        if first:
+            g.scalar.dma_start(T.ws[:], T.w[:]).then_inc(S.wld, 16)
+
+        col = (mem * G + gi) * NC
+        g.wait_ge(S.xld, 16)
+        g.remote_dma_fused(
+            [RemoteDMATransfer(dst_ids=[did(mine[k])], dma_engine_mask=bits(es[k * per:(k + 1) * per]),
+                               remote_sem=S.xarr, srcs=[T.xs[:, k * NC:(k + 1) * NC]],
+                               dsts=[T.land[:, col:col + NC]], alu_op=0)
+             for k in range(K)], local_sem=S.sent)
+        sent = per * K
+        if first:
+            s = wslot[gi]
+            g.wait_ge(S.wld, 16)
+            g.remote_dma_fused(
+                [RemoteDMATransfer(dst_ids=[did(c) for c in mine], dma_engine_mask=bits(es), remote_sem=S.wown,
+                                   srcs=[T.ws[:]], dsts=[T.wall[:, s * M:(s + 1) * M] for _ in mine], alu_op=0)],
+                local_sem=S.sent)
+            sent += len(es)
+
+        plane_ranks = [c for j, c in enumerate(cores) if pl[j] == p]
+        g.sync.wait_ge(S.yarr, sum(len(common(wk, plane_ranks)) for wk in mine))
+        g.sync.dma_start(T.y[:], T.ys[:]).then_inc(S.st, 16)
+        g.wait_ge(S.sent, sent)
+        g.wait_ge(S.st, 16)
+        return
+
+    where = [(k, p) for k in range(K) for p in range(2) if workers[k][p] == core]
+    if not where:
+        return
+    k, p = where[0]
+    mate = workers[k][1 - p]
+    ranks_here = [c for j, c in enumerate(cores) if pl[j] == p]
+    own_g = [gi for gi in range(G) if pl[groups[gi][0]] == p]
+    far_g = [gi for gi in range(G) if pl[groups[gi][0]] != p]
+    W = G * NC
+    V, TE = g.vector, g.tensor
+
+    def x_engines(c):
+        return len(common(c, [workers[kk][p] for kk in range(K)]))
+
+    n_x = sum(x_engines(c) // K for c in ranks_here)
+    n_wown = sum(x_engines(cores[groups[gi][0]]) for gi in own_g)
+    es_m = common(core, [mate])
+    es_r = common(core, ranks_here)
+
+    V.memset(T.zero[:], 0.0).then_inc(S.vz, 1)
+
+    g.wait_ge(S.xarr, n_x)
+    g.remote_dma_fused(
+        [RemoteDMATransfer(dst_ids=[did(mate)], dma_engine_mask=bits(es_m), remote_sem=S.carr,
+                           srcs=[T.land[:, i * W:(i + 1) * W] for i in range(MEM)], dsts=[T.part[:]], alu_op=1)],
+        local_sem=S.sent)
+    lo = min(wslot[gi] for gi in own_g) * M
+    hi = (max(wslot[gi] for gi in own_g) + 1) * M
+    g.wait_ge(S.wown, n_wown)
+    g.remote_dma_fused(
+        [RemoteDMATransfer(dst_ids=[did(mate)], dma_engine_mask=bits(es_m), remote_sem=S.wmate,
+                           srcs=[T.wall[:, lo:hi]], dsts=[T.wall[:, lo:hi]], alu_op=0)],
+        local_sem=S.sent)
+
+    V.wait_ge(S.xarr, n_x)
+    V.tensor_tensor(T.own[:], T.land[:, 0:W], T.land[:, W:2 * W], AluOpType.add).then_inc(S.va, 1)
+    V.wait_ge(S.vz, 1)
+    V.wait_ge(S.va, 1)
+    V.tensor_tensor(T.neg[:, 0:W], T.zero[:], T.own[:], AluOpType.subtract).then_inc(S.vn, 1)
+
+    def mm(gi, rhs, start, stop):
+        s = wslot[gi]
+        return TE.matmul(T.acc[:, 0:NC], T.wall[:, s * M:(s + 1) * M], rhs[:, gi * NC:(gi + 1) * NC], start, stop)
+
+    TE.wait_ge(S.va, 1)
+    TE.wait_ge(S.wown, n_wown)
+    for i, gi in enumerate(own_g):
+        mm(gi, T.own, i == 0, False)
+
+    V.wait_ge(S.vn, 1)
+    V.wait_ge(S.carr, len(es_m))
+    V.tensor_tensor(T.top[:], T.part[:], T.neg[:, 0:W], AluOpType.max).then_inc(S.vt, 1)
+
+    TE.wait_ge(S.vt, 1)
+    for gi in own_g:
+        mm(gi, T.top, False, False)
+    TE.wait_ge(S.wmate, len(es_m))
+    for gi in far_g:
+        mm(gi, T.own, False, False)
+    for i, gi in enumerate(far_g):
+        last = i == len(far_g) - 1
+        ins = mm(gi, T.top, False, last)
+        if last:
+            ins.then_inc(S.mm, 1)
+
+    V.wait_ge(S.mm, 1)
+    V.tensor_copy(T.res[:], T.acc[:, 0:NC]).then_inc(S.vr, 1)
+
+    g.wait_ge(S.vr, 1)
+    g.remote_dma_fused(
+        [RemoteDMATransfer(dst_ids=[did(c) for c in ranks_here], dma_engine_mask=bits(es_r), remote_sem=S.yarr,
+                           srcs=[T.res[:]], dsts=[T.ys[:, k * NC:(k + 1) * NC] for _ in ranks_here], alu_op=0)],
+        local_sem=S.sent)
+    g.wait_ge(S.sent, 2 * len(es_m) + len(es_r))

@@ -6,7 +6,7 @@ F = 256
 M = 128
 G = 3
 MEM = 2
-K = 2
+K = 4
 NC = F // K
 
 SCRATCH = {
@@ -106,7 +106,7 @@ def rank_program(g, core, T, topo):
             sent += len(es)
 
         plane_ranks = [c for j, c in enumerate(cores) if pl[j] == p]
-        g.sync.wait_ge(S.yarr, sum(len(common(wk, plane_ranks)) for wk in mine))
+        g.sync.wait_ge(S.yarr, sum(len(common(wk, [c for c in plane_ranks])) for wk in mine))
         g.sync.dma_start(T.y[:], T.ys[:]).then_inc(S.st, 16)
         g.wait_ge(S.sent, sent)
         g.wait_ge(S.st, 16)

from concourse.bass import DstId, RemoteDMATransfer
from concourse.mybir import AluOpType

P = 128
F = 256
M = 128
G = 3
MEM = 2
K = 4
NC = F // K

SCRATCH = {
    "xs": ("sbuf", [P, F], "bfloat16"),
    "ws": ("sbuf", [P, M], "bfloat16"),
    "ys": ("sbuf", [P, F], "bfloat16"),
    "land": ("sbuf", [P, MEM * G * NC], "bfloat16"),
    "part": ("sbuf", [P, G * NC], "bfloat16"),
    "wall": ("sbuf", [P, G * M], "bfloat16"),
    "zero": ("sbuf", [P, G * NC], "bfloat16"),
    "own": ("sbuf", [P, G * NC], "bfloat16"),
    "top": ("sbuf", [P, G * NC], "bfloat16"),
    "res": ("sbuf", [P, NC], "bfloat16"),
    "neg": ("psum", [P, 512], "float32"),
    "acc": ("psum", [P, 512], "float32"),
}
SEMAPHORES = ["xld", "wld", "st", "sent", "xarr", "wown", "wmate", "carr", "yarr",
              "vz", "va", "vn", "vt", "mm", "vr"]


def _plan(T, topo):
    cores = list(T.cores)
    groups = T.tables["GROUPS"]
    chips = [topo.chip(c) for c in cores]
    reps = []
    pl = []
    for ch in chips:
        hit = [i for i, r in enumerate(reps) if r == ch or topo.same_plane(r, ch)]
        if not hit:
            reps.append(ch)
            hit = [len(reps) - 1]
        pl.append(hit[0])
    assert len(reps) == 2
    pairs = [(a, b) for a in range(len(cores)) if pl[a] == 0
             for b in range(len(cores)) if topo.mates(chips[a], chips[b])]
    every = range(topo.CHIPS * topo.CORES_PER_CHIP)
    workers = []
    for a, b in pairs[:K]:
        two = []
        for r, q in ((a, b), (b, a)):
            two.append([c for c in every
                        if topo.chip(c) == chips[r] and T.rank_of(c) is None
                        and topo.may_write(c, cores[q]) and topo.die(c) == topo.die(cores[r])][0])
        workers.append(two)
    order = sorted(range(len(groups)), key=lambda gi: (pl[groups[gi][0]], gi))
    wslot = [order.index(gi) for gi in range(len(groups))]
    return cores, groups, pl, workers, wslot


def rank_program(g, core, T, topo):
    cores, groups, pl, workers, wslot = _plan(T, topo)
    S = T.sem

    def did(c):
        rid, pid, _ = topo.addr(c)
        return DstId(rid=rid, pnc=pid)

    def common(src, dsts):
        m = topo.mask(src, dsts[0])
        for d in dsts[1:]:
            m &= topo.mask(src, d)
        return [e for e in range(m.bit_length()) if (m >> e) & 1]

    def bits(es):
        return sum(1 << e for e in es)

    rank = T.rank_of(core)

    if rank is not None:
        p = pl[rank]
        gi = [i for i, gr in enumerate(groups) if rank in gr][0]
        mem = [j for j in groups[gi] if pl[j] == p].index(rank)
        first = groups[gi][0] == rank
        mine = [workers[k][p] for k in range(K)]
        es = common(core, mine)
        per = len(es) // K

        g.sync.dma_start(T.xs[:], T.x[:]).then_inc(S.xld, 16)
        if first:
            g.scalar.dma_start(T.ws[:], T.w[:]).then_inc(S.wld, 16)

        col = (mem * G + gi) * NC
        g.wait_ge(S.xld, 16)
        g.remote_dma_fused(
            [RemoteDMATransfer(dst_ids=[did(mine[k])], dma_engine_mask=bits(es[k * per:(k + 1) * per]),
                               remote_sem=S.xarr, srcs=[T.xs[:, k * NC:(k + 1) * NC]],
                               dsts=[T.land[:, col:col + NC]], alu_op=0)
             for k in range(K)], local_sem=S.sent)
        sent = per * K
        if first:
            s = wslot[gi]
            g.wait_ge(S.wld, 16)
            g.remote_dma_fused(
                [RemoteDMATransfer(dst_ids=[did(c) for c in mine], dma_engine_mask=bits(es), remote_sem=S.wown,
                                   srcs=[T.ws[:]], dsts=[T.wall[:, s * M:(s + 1) * M] for _ in mine], alu_op=0)],
                local_sem=S.sent)
            sent += len(es)

        plane_ranks = [c for j, c in enumerate(cores) if pl[j] == p]
        g.sync.wait_ge(S.yarr, sum(len(common(wk, [c for c in plane_ranks])) for wk in mine))
        g.sync.dma_start(T.y[:], T.ys[:]).then_inc(S.st, 16)
        g.wait_ge(S.sent, sent)
        g.wait_ge(S.st, 16)
        return

    where = [(k, p) for k in range(K) for p in range(2) if workers[k][p] == core]
    if not where:
        return
    k, p = where[0]
    mate = workers[k][1 - p]
    ranks_here = [c for j, c in enumerate(cores) if pl[j] == p]
    own_g = [gi for gi in range(G) if pl[groups[gi][0]] == p]
    far_g = [gi for gi in range(G) if pl[groups[gi][0]] != p]
    W = G * NC
    V, TE = g.vector, g.tensor

    def x_engines(c):
        return len(common(c, [workers[kk][p] for kk in range(K)]))

    n_x = sum(x_engines(c) // K for c in ranks_here)
    n_wown = sum(x_engines(cores[groups[gi][0]]) for gi in own_g)
    es_m = common(core, [mate])
    es_r = common(core, ranks_here)

    V.memset(T.zero[:], 0.0).then_inc(S.vz, 1)

    g.wait_ge(S.xarr, n_x)
    g.remote_dma_fused(
        [RemoteDMATransfer(dst_ids=[did(mate)], dma_engine_mask=bits(es_m), remote_sem=S.carr,
                           srcs=[T.land[:, i * W:(i + 1) * W] for i in range(MEM)], dsts=[T.part[:]], alu_op=1)],
        local_sem=S.sent)
    lo = min(wslot[gi] for gi in own_g) * M
    hi = (max(wslot[gi] for gi in own_g) + 1) * M
    g.wait_ge(S.wown, n_wown)
    g.remote_dma_fused(
        [RemoteDMATransfer(dst_ids=[did(mate)], dma_engine_mask=bits(es_m), remote_sem=S.wmate,
                           srcs=[T.wall[:, lo:hi]], dsts=[T.wall[:, lo:hi]], alu_op=0)],
        local_sem=S.sent)

    V.wait_ge(S.xarr, n_x)
    V.tensor_tensor(T.own[:], T.land[:, 0:W], T.land[:, W:2 * W], AluOpType.add).then_inc(S.va, 1)
    V.wait_ge(S.vz, 1)
    V.wait_ge(S.va, 1)
    V.tensor_tensor(T.neg[:, 0:W], T.zero[:], T.own[:], AluOpType.subtract).then_inc(S.vn, 1)

    def mm(gi, rhs, start, stop):
        s = wslot[gi]
        return TE.matmul(T.acc[:, 0:NC], T.wall[:, s * M:(s + 1) * M], rhs[:, gi * NC:(gi + 1) * NC], start, stop)

    TE.wait_ge(S.va, 1)
    TE.wait_ge(S.wown, n_wown)
    for i, gi in enumerate(own_g):
        mm(gi, T.own, i == 0, False)

    V.wait_ge(S.vn, 1)
    V.wait_ge(S.carr, len(es_m))
    V.tensor_tensor(T.top[:], T.part[:], T.neg[:, 0:W], AluOpType.max).then_inc(S.vt, 1)

    TE.wait_ge(S.vt, 1)
    for gi in own_g:
        mm(gi, T.top, False, False)
    TE.wait_ge(S.wmate, len(es_m))
    for gi in far_g:
        mm(gi, T.own, False, False)
    for i, gi in enumerate(far_g):
        last = i == len(far_g) - 1
        ins = mm(gi, T.top, False, last)
        if last:
            ins.then_inc(S.mm, 1)

    V.wait_ge(S.mm, 1)
    V.tensor_copy(T.res[:], T.acc[:, 0:NC]).then_inc(S.vr, 1)

    g.wait_ge(S.vr, 1)
    g.remote_dma_fused(
        [RemoteDMATransfer(dst_ids=[did(c) for c in ranks_here], dma_engine_mask=bits(es_r), remote_sem=S.yarr,
                           srcs=[T.res[:]], dsts=[T.ys[:, k * NC:(k + 1) * NC] for _ in ranks_here], alu_op=0)],
        local_sem=S.sent)
    g.wait_ge(S.sent, 2 * len(es_m) + len(es_r))
